import numpy as np
import ml_dtypes


def mxq(x, axis, fmt="e4m3"):
    dtype, down = {"e4m3": (ml_dtypes.float8_e4m3fn, 7), "e5m2": (ml_dtypes.float8_e5m2, 14)}[fmt]
    v = np.moveaxis(np.asarray(x, np.float32).astype(ml_dtypes.bfloat16).astype(np.float64), axis, -1)
    blocks = v.reshape(v.shape[:-1] + (-1, 32))
    amax = np.abs(blocks).max(-1, keepdims=True)
    byte = np.maximum(np.where(amax > 0, np.frexp(amax)[1] - 1 + 127, 0) - down, 1)
    scale = np.exp2(byte - 127.0)
    codes = (blocks / scale).astype(np.float32).astype(dtype).astype(np.float64)
    return np.moveaxis((codes * scale).reshape(v.shape), -1, axis)


WIDE = False


def mx_kscale(k):
    if not WIDE:
        return np.ones(k)
    levels = np.array([10, -10, 5, -5, 0])
    if k % 512:
        return np.exp2(np.random.permutation(np.resize(levels, k // 32))).repeat(32)
    a = np.empty((k // 512, 16))
    for p in range(k // 512):
        a[p, :8] = np.random.permutation(np.resize(levels, 8))
        for g in range(8):
            far = levels[np.abs(levels - a[p, g]) >= 10]
            a[p, g + 8] = far[np.random.randint(len(far))]
    return np.exp2(a.ravel()).repeat(32)


def f64(x):
    return np.asarray(x).astype(np.float64)


def striped8(idx):
    return np.concatenate([x.reshape(-1, 16).T for x in idx]).astype(np.uint16)


def runs(offs, k):
    lists = np.stack([offs[16 * r : 16 * r + 16].T.reshape(-1) for r in range(8)]).astype(np.int64)
    return lists[np.arange(k) % 512 // 64]


def pack_weight(w):
    k, n = w.shape
    w = f64(np.asarray(w, np.float32).astype(ml_dtypes.bfloat16)).reshape(k // 32, 32, n)
    amax = np.abs(w).max(1)
    byte = np.clip(np.where(amax > 0, np.frexp(amax)[1] - 1 + 127 - 7, 1), 1, 254)
    scaled = (w * np.exp2(127.0 - byte)[:, None, :]).reshape(k, n).astype(np.float32)
    words = np.ascontiguousarray(scaled.reshape(k // 512, 128, 4, n).transpose(0, 1, 3, 2)).astype(ml_dtypes.float8_e4m3fn).view(np.uint8)
    return words, np.ascontiguousarray(byte.astype(np.uint8).reshape(k // 512, 16, n))


def unpack_weight(words, scales):
    g, p, n, _ = words.shape
    vals = np.ascontiguousarray(words).view(ml_dtypes.float8_e4m3fn).astype(np.float64) * np.repeat(np.exp2(scales.astype(np.float64) - 127.0), 8, axis=1)[..., None]
    return vals.transpose(0, 1, 3, 2).reshape(g * 512, n)


def relu(v):
    return np.maximum(v, 0.0)


K, T, S, N, H = 512, 2048, 512, 512, 512


def setup_inputs():
    n = np.random.standard_normal
    s = mx_kscale(K)[:, None]
    u = mx_kscale(H)
    packed_xT = pack_weight(n((K, T)) * s)
    return {
        "x_words": packed_xT[0],
        "x_scales": packed_xT[1],
        "w1": (n((K, H)) / np.sqrt(K) / s).astype(np.float32),
        "gn": (np.random.uniform(0.5, 1.5, (H, 1)) * u[:, None]).astype(np.float32),
        "w2": (n((H, N)) / np.sqrt(H) / u[:, None]).astype(np.float32),
        "offs": striped8(np.random.randint(0, T, (8, S))),
        "n1": striped8(np.stack([np.random.permutation(S) for _ in range(8)])),
        "n2": striped8(np.stack([np.random.permutation(S) for _ in range(8)])),
        "n3": striped8(np.stack([np.random.permutation(S) for _ in range(8)])),
        "n4": striped8(np.stack([np.random.permutation(S) for _ in range(8)])),
    }


def reference(x_words, x_scales, w1, gn, w2, offs, n1, n2, n3, n4):
    xq = unpack_weight(x_words, x_scales)[np.arange(K)[:, None], runs(offs, K)]
    y = mxq(f64(w1), 0, "e4m3").T @ xq
    pa = y - (y[np.arange(H)[:, None], runs(n1, H)])
    pb = y[np.arange(H)[:, None], runs(n2, H)] - y
    z = f64(gn) * (relu(np.minimum(pa, pb)) - (relu(-1.0 * np.maximum(pa, pb))))
    h = mxq(f64(w2), 0, "e4m3").T @ mxq(z, 0, "e4m3")
    st = h - (h[np.arange(N)[:, None], runs(n3, N)])
    return np.maximum(st, st[np.arange(N)[:, None], runs(n4, N)])

@@ -1,0 +1,199 @@
+from contextlib import ExitStack
+
+import concourse.mybir as mybir
+
+K, T, S, H, N = 512, 2048, 512, 512, 512
+FLOPS = 2 * K * H * S + 2 * H * N * S
+
+F32 = mybir.dt.float32
+BF16 = mybir.dt.bfloat16
+I32 = mybir.dt.int32
+U32 = mybir.dt.uint32
+U16 = mybir.dt.uint16
+U8 = mybir.dt.uint8
+FP8X4 = mybir.dt.float8_e4m3fn_x4
+ALU = mybir.AluOpType
+COPY = mybir.ActivationFunctionType.Copy
+
+P = 128
+PACK = 4
+HALF = S // 2
+LIST_COLS = S // 16
+W1_VECTOR_SHARE = 84
+
+
+def deal_columns(engine_copy, grouped, raw, m0, m1):
+    engine_copy(
+        grouped[:].rearrange("p (t m j) -> p m t j", t=PACK, j=PACK)[:, m0:m1],
+        raw[:].rearrange("p j (m t) -> p m t j", t=PACK)[:, m0:m1],
+    )
+
+
+def tile_picked_hashminmodhopmx_none_p_kernel(
+    tc, x_words, x_scales, w1, gn, w2, offs, n1, n2, n3, n4, out
+):
+    nc = tc.nc
+    with ExitStack() as ctx:
+        keep = ctx.enter_context(tc.tile_pool(name="keep", bufs=1))
+        ring = ctx.enter_context(tc.tile_pool(name="ring", bufs=2))
+        psum = ctx.enter_context(tc.psum_pool(name="psum", bufs=1))
+
+        def load_list(src, name):
+            tile = keep.tile([P, LIST_COLS], U16, name=name)
+            nc.sync.dma_start(tile[:], src)
+            return tile
+
+        def half_list(tile, c):
+            return tile[:, c * LIST_COLS // 2 : (c + 1) * LIST_COLS // 2]
+
+        def cols(c):
+            return slice(c * HALF, (c + 1) * HALF)
+
+        scale_table = keep.tile([P, T], U8, name="scale_table")
+        nc.gpsimd.memset(scale_table[:].bitcast(I32), 0)
+        nc.scalar.dma_start(scale_table[:].bitcast(I32)[0:P:8, :], x_scales[0].bitcast(I32))
+
+        warm_in = keep.tile([P, 1], F32, name="warm_in")
+        warm_out = keep.tile([P, 1], F32, name="warm_out")
+        nc.vector.memset(warm_in[:], 0.0)
+        nc.scalar.activation(warm_out[:], warm_in[:], COPY)
+
+        offs_t = load_list(offs, "offs_t")
+        w1_raw = keep.tile([P, PACK, H], F32, name="w1_raw", tag="w_raw")
+        nc.sync.dma_start(w1_raw[:], w1.rearrange("(p j) c -> p j c", j=PACK))
+        n1_t = load_list(n1, "n1_t")
+        n2_t = load_list(n2, "n2_t")
+        word_table = keep.tile([P, T], U32, name="word_table")
+        nc.sync.dma_start(word_table[:].bitcast(I32), x_words[0].rearrange("p n t -> p (n t)").bitcast(I32))
+        n3_t = load_list(n3, "n3_t")
+        n4_t = load_list(n4, "n4_t")
+        gain = keep.tile([P, PACK], F32, name="gain")
+        nc.scalar.dma_start(gain[:], gn.rearrange("(p t) o -> p (t o)", t=PACK))
+
+        picked_scales = keep.tile([P, S], U8, name="picked_scales")
+        nc.vector.tensor_copy(picked_scales[:], scale_table[:].indirect(offs_t[:]))
+        x_plane = keep.tile([P, S], U8, name="x_plane", align_bytes=64)
+        nc.vector.tensor_copy(x_plane[:].bitcast(I32), picked_scales[:].bitcast(I32))
+        for i in range(1, 4):
+            nc.scalar.dma_start(x_plane[:].bitcast(I32)[i:P:32, :], picked_scales[:].bitcast(I32)[8 * i : P : 32, :])
+
+        neg_gain = keep.tile([P, PACK], F32, name="neg_gain")
+        nc.vector.tensor_scalar(neg_gain[:], gain[:], -1.0, None, ALU.mult)
+
+        w1_grouped = keep.tile([P, PACK * H], BF16, name="w1_grouped", align_bytes=64)
+        deal_columns(nc.vector.tensor_copy, w1_grouped, w1_raw, 0, W1_VECTOR_SHARE)
+        deal_columns(nc.scalar.copy, w1_grouped, w1_raw, W1_VECTOR_SHARE, P)
+        w1_codes = keep.tile([P, H], U32, name="w1_codes", align_bytes=64)
+        w1_plane = keep.tile([P, H], U8, name="w1_plane", align_bytes=64)
+        nc.vector.quantize_mx(out=w1_codes[:].bitcast(FP8X4), scales=w1_plane[:], in_=w1_grouped[:])
+
+        w2_raw = keep.tile([P, PACK, N], F32, name="w2_raw", tag="w_raw")
+        nc.sync.dma_start(w2_raw[:], w2.rearrange("(p j) c -> p j c", j=PACK))
+
+        x_codes = keep.tile([P, S], U32, name="x_codes", align_bytes=64)
+        for c in range(2):
+            nc.vector.tensor_copy(x_codes[:, cols(c)], word_table[:].indirect(half_list(offs_t, c)))
+
+        def product(bank, codes, plane, t, rhs, rhs_plane):
+            nc.tensor.matmul_mx(
+                out=bank[:],
+                lhsT=codes[:, t * P : (t + 1) * P].bitcast(FP8X4),
+                lhsT_scale=plane[:, t * P : (t + 1) * P],
+                rhs=rhs.bitcast(FP8X4),
+                rhs_scale=rhs_plane,
+                start=True,
+                stop=True,
+            )
+
+        y_pos = [keep.tile([P, S], F32, name="y_pos%d" % t) for t in range(PACK)]
+        y_neg = [keep.tile([P, S], F32, name="y_neg%d" % t) for t in range(PACK)]
+        pieces = [(0, cols(0), 0), (0, cols(1), PACK)] + [(t, slice(0, S), t) for t in range(1, PACK)]
+        for t, cs, b in pieces:
+            bank = psum.tile([P, cs.stop - cs.start], F32, name="y_bank", tag="bank%d" % b)
+            product(bank, w1_codes, w1_plane, t, x_codes[:, cs], x_plane[:, cs])
+            nc.scalar.activation(y_pos[t][:, cs], bank[:], COPY, scale=gain[:, t : t + 1])
+            nc.scalar.activation(y_neg[t][:, cs], bank[:], COPY, scale=neg_gain[:, t : t + 1])
+
+        w2_grouped = keep.tile([P, PACK * N], BF16, name="w2_grouped", align_bytes=64)
+        deal_columns(nc.scalar.copy, w2_grouped, w2_raw, 0, P // 2)
+        deal_columns(nc.scalar.copy, w2_grouped, w2_raw, P // 2, P)
+        w2_codes = keep.tile([P, N], U32, name="w2_codes", align_bytes=64)
+        w2_plane = keep.tile([P, N], U8, name="w2_plane", align_bytes=64)
+
+        h_neg = [keep.tile([P, 2 * S], F32, name="h_neg%d" % t) for t in range(PACK)]
+        st = [keep.tile([P, 2 * S], F32, name="st%d" % t) for t in range(PACK)]
+        z_planes = [keep.tile([P, PACK, HALF], BF16, name="z_planes%d" % c) for c in range(2)]
+
+        def floor_buf(c, t):
+            return h_neg[t][:, S + c * HALF : S + (c + 1) * HALF]
+
+        def second_product(c, interleave):
+            grouped = keep.tile([P, HALF * PACK], BF16, name="z_grouped%d" % c, align_bytes=64)
+            interleave(grouped[:].rearrange("p (j t) -> p j t", t=PACK), z_planes[c][:].rearrange("p t j -> p j t"))
+            return grouped
+
+        def quantize_and_multiply(c, grouped):
+            codes = keep.tile([P, HALF], U32, name="z_codes%d" % c, align_bytes=64)
+            plane = keep.tile([P, HALF], U8, name="z_plane%d" % c, align_bytes=64)
+            nc.vector.quantize_mx(out=codes[:].bitcast(FP8X4), scales=plane[:], in_=grouped[:])
+            for t in range(PACK):
+                bank = psum.tile([P, HALF], F32, name="h_bank", tag="bank%d" % (PACK * c + t))
+                product(bank, w2_codes, w2_plane, t, codes[:], plane[:])
+                nc.scalar.activation(h_neg[t][:, cols(c)], bank[:], COPY, scale=-1.0)
+                nc.scalar.copy(st[t][:, S + c * HALF : S + (c + 1) * HALF], bank[:])
+
+        steps = [(c, t) for c in range(2) for t in range(PACK)]
+        pa, pb = {}, {}
+
+        def lower(c, t):
+            nc.vector.scalar_tensor_tensor(floor_buf(c, t), pb[c, t][:], 0.0, pa[c, t][:], ALU.min, ALU.max)
+
+        def upper(c, t):
+            nc.vector.scalar_tensor_tensor(z_planes[c][:, t, :], pb[c, t][:], 0.0, floor_buf(c, t), ALU.max, ALU.min)
+
+        for s, (c, t) in enumerate(steps):
+            pa[c, t] = ring.tile([P, HALF], F32, name="pa")
+            nc.vector.tensor_tensor(pa[c, t][:], y_neg[t][:].indirect(half_list(n1_t, c)), y_pos[t][:, cols(c)], ALU.add)
+            if s > 0:
+                lower(*steps[s - 1])
+            pb[c, t] = ring.tile([P, HALF], F32, name="pb")
+            nc.vector.tensor_tensor(pb[c, t][:], y_pos[t][:].indirect(half_list(n2_t, c)), y_neg[t][:, cols(c)], ALU.add)
+            if s > 0:
+                upper(*steps[s - 1])
+            if s == PACK:
+                grouped0 = second_product(0, nc.scalar.copy)
+                nc.vector.quantize_mx(out=w2_codes[:].bitcast(FP8X4), scales=w2_plane[:], in_=w2_grouped[:])
+            if s == PACK + 1:
+                quantize_and_multiply(0, grouped0)
+        lower(*steps[-1])
+        upper(*steps[-1])
+        quantize_and_multiply(1, second_product(1, nc.vector.tensor_copy))
+
+        out_rows = out.rearrange("(p t) j -> p t j", t=PACK)
+        far = {}
+
+        def difference(t):
+            nc.vector.tensor_tensor(st[t][:, 0:S], h_neg[t][:].indirect(n3_t[:]), st[t][:, S : 2 * S], ALU.add)
+
+        def fetch(t, cs, offsets):
+            far[t, cs.start] = ring.tile([P, cs.stop - cs.start], F32, name="far")
+            nc.vector.tensor_copy(far[t, cs.start][:], st[t][:].indirect(offsets))
+
+        def finish(t, cs):
+            res = ring.tile([P, cs.stop - cs.start], F32, name="res", bufs=3)
+            nc.vector.tensor_tensor(res[:], far[t, cs.start][:], st[t][:, cs], ALU.max)
+            nc.sync.dma_start(out_rows[:, t, cs], res[:])
+
+        whole = slice(0, S)
+        difference(0)
+        for t in range(PACK - 1):
+            difference(t + 1)
+            if t > 0:
+                finish(t - 1, whole)
+            fetch(t, whole, n4_t[:])
+        last = PACK - 1
+        fetch(last, cols(0), half_list(n4_t, 0))
+        finish(last - 1, whole)
+        fetch(last, cols(1), half_list(n4_t, 1))
+        finish(last, cols(0))
+        finish(last, cols(1))

@@ -49,13 +49,13 @@ def tile_picked_hashminmodhopmx_none_p_kernel(
         def cols(c):
             return slice(c * HALF, (c + 1) * HALF)
 
-        scale_table = keep.tile([P, T], U8, name="scale_table")
+        scale_table = keep.tile([P, T], U8, name="scale_table", tag="early", align_bytes=64)
         nc.gpsimd.memset(scale_table[:].bitcast(I32), 0)
         nc.scalar.dma_start(scale_table[:].bitcast(I32)[0:P:8, :], x_scales[0].bitcast(I32))
 
         warm_in = keep.tile([P, 1], F32, name="warm_in")
         warm_out = keep.tile([P, 1], F32, name="warm_out")
-        nc.vector.memset(warm_in[:], 0.0)
+        nc.gpsimd.memset(warm_in[:], 0.0)
         nc.scalar.activation(warm_out[:], warm_in[:], COPY)
 
         offs_t = load_list(offs, "offs_t")
@@ -68,19 +68,23 @@ def tile_picked_hashminmodhopmx_none_p_kernel(
         n3_t = load_list(n3, "n3_t")
         n4_t = load_list(n4, "n4_t")
         gain = keep.tile([P, PACK], F32, name="gain")
-        nc.scalar.dma_start(gain[:], gn.rearrange("(p t) o -> p (t o)", t=PACK))
+        nc.gpsimd.dma_start(gain[:], gn.rearrange("(p t) o -> p (t o)", t=PACK))
 
         picked_scales = keep.tile([P, S], U8, name="picked_scales")
         nc.vector.tensor_copy(picked_scales[:], scale_table[:].indirect(offs_t[:]))
         x_plane = keep.tile([P, S], U8, name="x_plane", align_bytes=64)
-        nc.vector.tensor_copy(x_plane[:].bitcast(I32), picked_scales[:].bitcast(I32))
-        for i in range(1, 4):
+        nc.vector.memset(x_plane[:].bitcast(I32), 0)
+        for i in range(4):
             nc.scalar.dma_start(x_plane[:].bitcast(I32)[i:P:32, :], picked_scales[:].bitcast(I32)[8 * i : P : 32, :])
+
+        negated = [keep.tile([P, 2 * S], F32, name="negated%d" % t) for t in range(PACK)]
+        for t in range(PACK):
+            nc.vector.memset(negated[t][:, S : 2 * S], 0.0)
 
         neg_gain = keep.tile([P, PACK], F32, name="neg_gain")
         nc.vector.tensor_scalar(neg_gain[:], gain[:], -1.0, None, ALU.mult)
 
-        w1_grouped = keep.tile([P, PACK * H], BF16, name="w1_grouped", align_bytes=64)
+        w1_grouped = keep.tile([P, PACK * H], BF16, name="w1_grouped", tag="early", align_bytes=64)
         deal_columns(nc.vector.tensor_copy, w1_grouped, w1_raw, 0, W1_VECTOR_SHARE)
         deal_columns(nc.scalar.copy, w1_grouped, w1_raw, W1_VECTOR_SHARE, P)
         w1_codes = keep.tile([P, H], U32, name="w1_codes", align_bytes=64)
@@ -105,75 +109,102 @@ def tile_picked_hashminmodhopmx_none_p_kernel(
                 stop=True,
             )
 
-        y_pos = [keep.tile([P, S], F32, name="y_pos%d" % t) for t in range(PACK)]
-        y_neg = [keep.tile([P, S], F32, name="y_neg%d" % t) for t in range(PACK)]
-        pieces = [(0, cols(0), 0), (0, cols(1), PACK)] + [(t, slice(0, S), t) for t in range(1, PACK)]
-        for t, cs, b in pieces:
-            bank = psum.tile([P, cs.stop - cs.start], F32, name="y_bank", tag="bank%d" % b)
-            product(bank, w1_codes, w1_plane, t, x_codes[:, cs], x_plane[:, cs])
-            nc.scalar.activation(y_pos[t][:, cs], bank[:], COPY, scale=gain[:, t : t + 1])
-            nc.scalar.activation(y_neg[t][:, cs], bank[:], COPY, scale=neg_gain[:, t : t + 1])
+        def leave_bank(on_vector, dst, bank, factor):
+            if on_vector:
+                nc.vector.tensor_scalar(dst, bank[:], factor, None, ALU.mult)
+            else:
+                nc.scalar.activation(dst, bank[:], COPY, scale=factor)
 
-        w2_grouped = keep.tile([P, PACK * N], BF16, name="w2_grouped", align_bytes=64)
+        quarter = S // 4
+        pieces = [(0, slice(0, HALF), False), (0, slice(HALF, HALF + quarter), False), (0, slice(HALF + quarter, S), True)]
+        pieces = pieces + [(t, slice(0, S), False) for t in range(1, PACK)]
+
+        def project(which, codes, plane, rhs, rhs_plane, pos, pos_factor, neg_factor):
+            for b in which:
+                t, cs, on_vector = pieces[b]
+                bank = psum.tile([P, cs.stop - cs.start], F32, name="bank", tag="bank%d" % b)
+                product(bank, codes, plane, t, rhs[:, cs], rhs_plane[:, cs])
+                leave_bank(on_vector, negated[t][:, cs], bank, neg_factor(t))
+                leave_bank(on_vector, pos(t)[:, cs], bank, pos_factor(t))
+
+        y_pos = [keep.tile([P, S], F32, name="y_pos%d" % t) for t in range(PACK)]
+        project(
+            range(len(pieces)), w1_codes, w1_plane, x_codes, x_plane,
+            lambda t: y_pos[t][:], lambda t: gain[:, t : t + 1], lambda t: neg_gain[:, t : t + 1],
+        )
+
+        w2_grouped = keep.tile([P, PACK * N], BF16, name="w2_grouped", tag="late", align_bytes=64)
         deal_columns(nc.scalar.copy, w2_grouped, w2_raw, 0, P // 2)
         deal_columns(nc.scalar.copy, w2_grouped, w2_raw, P // 2, P)
         w2_codes = keep.tile([P, N], U32, name="w2_codes", align_bytes=64)
         w2_plane = keep.tile([P, N], U8, name="w2_plane", align_bytes=64)
 
-        h_neg = [keep.tile([P, 2 * S], F32, name="h_neg%d" % t) for t in range(PACK)]
-        st = [keep.tile([P, 2 * S], F32, name="st%d" % t) for t in range(PACK)]
-        z_planes = [keep.tile([P, PACK, HALF], BF16, name="z_planes%d" % c) for c in range(2)]
+        def bf16_half(name, c):
+            return keep.tile([P, HALF * PACK], BF16, name="%s%d" % (name, c), align_bytes=64)
 
-        def floor_buf(c, t):
-            return h_neg[t][:, S + c * HALF : S + (c + 1) * HALF]
-
-        def second_product(c, interleave):
-            grouped = keep.tile([P, HALF * PACK], BF16, name="z_grouped%d" % c, align_bytes=64)
-            interleave(grouped[:].rearrange("p (j t) -> p j t", t=PACK), z_planes[c][:].rearrange("p t j -> p j t"))
+        def round_and_interleave(name, c, planes):
+            grouped = bf16_half(name, c)
+            nc.scalar.copy(grouped[:].rearrange("p (j t) -> p j t", t=PACK), planes.rearrange("p t j -> p j t"))
             return grouped
 
-        def quantize_and_multiply(c, grouped):
-            codes = keep.tile([P, HALF], U32, name="z_codes%d" % c, align_bytes=64)
-            plane = keep.tile([P, HALF], U8, name="z_plane%d" % c, align_bytes=64)
-            nc.vector.quantize_mx(out=codes[:].bitcast(FP8X4), scales=plane[:], in_=grouped[:])
-            for t in range(PACK):
-                bank = psum.tile([P, HALF], F32, name="h_bank", tag="bank%d" % (PACK * c + t))
-                product(bank, w2_codes, w2_plane, t, codes[:], plane[:])
-                nc.scalar.activation(h_neg[t][:, cols(c)], bank[:], COPY, scale=-1.0)
-                nc.scalar.copy(st[t][:, S + c * HALF : S + (c + 1) * HALF], bank[:])
+        pa = keep.tile([P, PACK, S], F32, name="pa")
+        for t in range(PACK):
+            nc.vector.tensor_tensor(pa[:, t, :], negated[t][:].indirect(n1_t[:]), y_pos[t][:], ALU.add)
 
-        steps = [(c, t) for c in range(2) for t in range(PACK)]
-        pa, pb = {}, {}
+        def gather_pb(pb, c, t):
+            nc.vector.tensor_tensor(pb[:, t, :], y_pos[t][:].indirect(half_list(n2_t, c)), negated[t][:, cols(c)], ALU.add)
 
-        def lower(c, t):
-            nc.vector.scalar_tensor_tensor(floor_buf(c, t), pb[c, t][:], 0.0, pa[c, t][:], ALU.min, ALU.max)
+        pb0 = keep.tile([P, PACK, HALF], F32, name="pb0")
+        for t in range(PACK):
+            gather_pb(pb0, 0, t)
+        a0 = round_and_interleave("a", 0, pa[:, :, cols(0)])
+        b0 = round_and_interleave("b", 0, pb0[:])
+        a1 = round_and_interleave("a", 1, pa[:, :, cols(1)])
+        nc.vector.quantize_mx(out=w2_codes[:].bitcast(FP8X4), scales=w2_plane[:], in_=w2_grouped[:])
+        pb1 = keep.tile([P, PACK, HALF], F32, name="pb1", tag="late", align_bytes=64)
+        for t in range(PACK - 1):
+            gather_pb(pb1, 1, t)
 
-        def upper(c, t):
-            nc.vector.scalar_tensor_tensor(z_planes[c][:, t, :], pb[c, t][:], 0.0, floor_buf(c, t), ALU.max, ALU.min)
+        z_codes = keep.tile([P, S], U32, name="z_codes", align_bytes=64)
+        z_plane = keep.tile([P, S], U8, name="z_plane", align_bytes=64)
+        st = [keep.tile([P, 2 * S], F32, name="st%d" % t) for t in range(PACK)]
 
-        for s, (c, t) in enumerate(steps):
-            pa[c, t] = ring.tile([P, HALF], F32, name="pa")
-            nc.vector.tensor_tensor(pa[c, t][:], y_neg[t][:].indirect(half_list(n1_t, c)), y_pos[t][:, cols(c)], ALU.add)
-            if s > 0:
-                lower(*steps[s - 1])
-            pb[c, t] = ring.tile([P, HALF], F32, name="pb")
-            nc.vector.tensor_tensor(pb[c, t][:], y_pos[t][:].indirect(half_list(n2_t, c)), y_neg[t][:, cols(c)], ALU.add)
-            if s > 0:
-                upper(*steps[s - 1])
-            if s == PACK:
-                grouped0 = second_product(0, nc.scalar.copy)
-                nc.vector.quantize_mx(out=w2_codes[:].bitcast(FP8X4), scales=w2_plane[:], in_=w2_grouped[:])
-            if s == PACK + 1:
-                quantize_and_multiply(0, grouped0)
-        lower(*steps[-1])
-        upper(*steps[-1])
-        quantize_and_multiply(1, second_product(1, nc.vector.tensor_copy))
+        def bound(name, c, b, op):
+            res = bf16_half(name, c)
+            nc.vector.tensor_scalar(res[:], b[:], 0.0, None, op)
+            return res
+
+        def combine(name, c, x, y, op):
+            res = bf16_half(name, c)
+            nc.vector.tensor_tensor(res[:], x[:], y[:], op)
+            return res
+
+        def quantize_z(c, z):
+            nc.vector.quantize_mx(out=z_codes[:, cols(c)].bitcast(FP8X4), scales=z_plane[:, cols(c)], in_=z[:])
+
+        def project_h(which):
+            project(which, w2_codes, w2_plane, z_codes, z_plane, lambda t: st[t][:, S : 2 * S], lambda t: 1.0, lambda t: -1.0)
+
+        low0 = bound("low", 0, b0, ALU.min)
+        gather_pb(pb1, 1, PACK - 1)
+        b1 = round_and_interleave("b", 1, pb1[:])
+        raised0 = combine("raised", 0, a0, low0, ALU.max)
+        high0 = bound("high", 0, b0, ALU.max)
+        z0 = combine("z", 0, raised0, high0, ALU.min)
+        low1 = bound("low", 1, b1, ALU.min)
+        quantize_z(0, z0)
+        project_h([0])
+        raised1 = combine("raised", 1, a1, low1, ALU.max)
+        high1 = bound("high", 1, b1, ALU.max)
+        z1 = combine("z", 1, raised1, high1, ALU.min)
+        quantize_z(1, z1)
+        project_h(range(1, len(pieces)))
 
         out_rows = out.rearrange("(p t) j -> p t j", t=PACK)
         far = {}
 
         def difference(t):
-            nc.vector.tensor_tensor(st[t][:, 0:S], h_neg[t][:].indirect(n3_t[:]), st[t][:, S : 2 * S], ALU.add)
+            nc.vector.tensor_tensor(st[t][:, 0:S], negated[t][:].indirect(n3_t[:]), st[t][:, S : 2 * S], ALU.add)
 
         def fetch(t, cs, offsets):
             far[t, cs.start] = ring.tile([P, cs.stop - cs.start], F32, name="far")

@@ -50,53 +50,53 @@ def tile_picked_hashminmodhopmx_none_p_kernel(
             return slice(c * HALF, (c + 1) * HALF)
 
         scale_table = keep.tile([P, T], U8, name="scale_table", tag="early", align_bytes=64)
-        nc.gpsimd.memset(scale_table[:].bitcast(I32), 0)
-        nc.scalar.dma_start(scale_table[:].bitcast(I32)[0:P:8, :], x_scales[0].bitcast(I32))
+        nc.vector.memset(scale_table[:].bitcast(I32), 0)
+        offs_t = load_list(offs, "offs_t")
+        n1_t = load_list(n1, "n1_t")
+        n2_t = load_list(n2, "n2_t")
+        n3_t = load_list(n3, "n3_t")
+        n4_t = load_list(n4, "n4_t")
+        nc.sync.dma_start(scale_table[:].bitcast(I32)[0:P:8, :], x_scales[0].bitcast(I32))
+        w1_raw = keep.tile([P, PACK, H], F32, name="w1_raw", tag="w_raw")
+        nc.sync.dma_start(w1_raw[:], w1.rearrange("(p j) c -> p j c", j=PACK))
+        word_table = keep.tile([P, T], U32, name="word_table")
+        nc.sync.dma_start(word_table[:].bitcast(I32), x_words[0].rearrange("p n t -> p (n t)").bitcast(I32))
 
         warm_in = keep.tile([P, 1], F32, name="warm_in")
         warm_out = keep.tile([P, 1], F32, name="warm_out")
         nc.gpsimd.memset(warm_in[:], 0.0)
         nc.scalar.activation(warm_out[:], warm_in[:], COPY)
 
-        offs_t = load_list(offs, "offs_t")
-        w1_raw = keep.tile([P, PACK, H], F32, name="w1_raw", tag="w_raw")
-        nc.sync.dma_start(w1_raw[:], w1.rearrange("(p j) c -> p j c", j=PACK))
-        n1_t = load_list(n1, "n1_t")
-        n2_t = load_list(n2, "n2_t")
-        word_table = keep.tile([P, T], U32, name="word_table")
-        nc.sync.dma_start(word_table[:].bitcast(I32), x_words[0].rearrange("p n t -> p (n t)").bitcast(I32))
-        n3_t = load_list(n3, "n3_t")
-        n4_t = load_list(n4, "n4_t")
         gain = keep.tile([P, PACK], F32, name="gain")
-        nc.gpsimd.dma_start(gain[:], gn.rearrange("(p t) o -> p (t o)", t=PACK))
+        nc.sync.dma_start(gain[:], gn.rearrange("(p t) o -> p (t o)", t=PACK))
 
         picked_scales = keep.tile([P, S], U8, name="picked_scales")
         nc.vector.tensor_copy(picked_scales[:], scale_table[:].indirect(offs_t[:]))
         x_plane = keep.tile([P, S], U8, name="x_plane", align_bytes=64)
         nc.vector.memset(x_plane[:].bitcast(I32), 0)
         for i in range(4):
-            nc.scalar.dma_start(x_plane[:].bitcast(I32)[i:P:32, :], picked_scales[:].bitcast(I32)[8 * i : P : 32, :])
+            nc.sync.dma_start(x_plane[:].bitcast(I32)[i:P:32, :], picked_scales[:].bitcast(I32)[8 * i : P : 32, :])
 
         negated = [keep.tile([P, 2 * S], F32, name="negated%d" % t) for t in range(PACK)]
         for t in range(PACK):
             nc.vector.memset(negated[t][:, S : 2 * S], 0.0)
 
-        neg_gain = keep.tile([P, PACK], F32, name="neg_gain")
-        nc.vector.tensor_scalar(neg_gain[:], gain[:], -1.0, None, ALU.mult)
-
         w1_grouped = keep.tile([P, PACK * H], BF16, name="w1_grouped", tag="early", align_bytes=64)
         deal_columns(nc.vector.tensor_copy, w1_grouped, w1_raw, 0, W1_VECTOR_SHARE)
         deal_columns(nc.scalar.copy, w1_grouped, w1_raw, W1_VECTOR_SHARE, P)
+        neg_gain = keep.tile([P, PACK], F32, name="neg_gain")
+        nc.scalar.activation(neg_gain[:], gain[:], COPY, scale=-1.0)
         w1_codes = keep.tile([P, H], U32, name="w1_codes", align_bytes=64)
         w1_plane = keep.tile([P, H], U8, name="w1_plane", align_bytes=64)
         nc.vector.quantize_mx(out=w1_codes[:].bitcast(FP8X4), scales=w1_plane[:], in_=w1_grouped[:])
 
-        w2_raw = keep.tile([P, PACK, N], F32, name="w2_raw", tag="w_raw")
-        nc.sync.dma_start(w2_raw[:], w2.rearrange("(p j) c -> p j c", j=PACK))
-
         x_codes = keep.tile([P, S], U32, name="x_codes", align_bytes=64)
         for c in range(2):
             nc.vector.tensor_copy(x_codes[:, cols(c)], word_table[:].indirect(half_list(offs_t, c)))
+
+        w2_raw = keep.tile([P, PACK, N], F32, name="w2_raw", tag="w_raw")
+        nc.sync.dma_start(w2_raw[:], w2.rearrange("(p j) c -> p j c", j=PACK))
+
 
         def product(bank, codes, plane, t, rhs, rhs_plane):
             nc.tensor.matmul_mx(
@@ -133,7 +133,7 @@ def tile_picked_hashminmodhopmx_none_p_kernel(
             lambda t: y_pos[t][:], lambda t: gain[:, t : t + 1], lambda t: neg_gain[:, t : t + 1],
         )
 
-        w2_grouped = keep.tile([P, PACK * N], BF16, name="w2_grouped", tag="late", align_bytes=64)
+        w2_grouped = keep.tile([P, PACK * N], BF16, name="w2_grouped", align_bytes=64)
         deal_columns(nc.scalar.copy, w2_grouped, w2_raw, 0, P // 2)
         deal_columns(nc.scalar.copy, w2_grouped, w2_raw, P // 2, P)
         w2_codes = keep.tile([P, N], U32, name="w2_codes", align_bytes=64)
@@ -160,8 +160,13 @@ def tile_picked_hashminmodhopmx_none_p_kernel(
         a0 = round_and_interleave("a", 0, pa[:, :, cols(0)])
         b0 = round_and_interleave("b", 0, pb0[:])
         a1 = round_and_interleave("a", 1, pa[:, :, cols(1)])
-        nc.vector.quantize_mx(out=w2_codes[:].bitcast(FP8X4), scales=w2_plane[:], in_=w2_grouped[:])
-        pb1 = keep.tile([P, PACK, HALF], F32, name="pb1", tag="late", align_bytes=64)
+
+        def quantize_w2(lo, hi):
+            nc.vector.quantize_mx(
+                out=w2_codes[:, lo:hi].bitcast(FP8X4), scales=w2_plane[:, lo:hi], in_=w2_grouped[:, PACK * lo : PACK * hi]
+            )
+
+        pb1 = keep.tile([P, PACK, HALF], F32, name="pb1", tag="w_raw")
         for t in range(PACK - 1):
             gather_pb(pb1, 1, t)
 
@@ -191,13 +196,16 @@ def tile_picked_hashminmodhopmx_none_p_kernel(
         raised0 = combine("raised", 0, a0, low0, ALU.max)
         high0 = bound("high", 0, b0, ALU.max)
         z0 = combine("z", 0, raised0, high0, ALU.min)
+        quantize_w2(0, P)
         low1 = bound("low", 1, b1, ALU.min)
         quantize_z(0, z0)
         project_h([0])
         raised1 = combine("raised", 1, a1, low1, ALU.max)
         high1 = bound("high", 1, b1, ALU.max)
         z1 = combine("z", 1, raised1, high1, ALU.min)
+        quantize_w2(P, 2 * P)
         quantize_z(1, z1)
+        quantize_w2(2 * P, N)
         project_h(range(1, len(pieces)))
 
         out_rows = out.rearrange("(p t) j -> p t j", t=PACK)

@@ -1,6 +1,7 @@
 from contextlib import ExitStack
 
 import concourse.mybir as mybir
+from concourse.masks import make_identity
 
 K, T, S, H, N = 512, 2048, 512, 512, 512
 FLOPS = 2 * K * H * S + 2 * H * N * S
@@ -14,6 +15,7 @@ U8 = mybir.dt.uint8
 FP8X4 = mybir.dt.float8_e4m3fn_x4
 ALU = mybir.AluOpType
 COPY = mybir.ActivationFunctionType.Copy
+RELU = mybir.ActivationFunctionType.Relu
 
 P = 128
 PACK = 4
@@ -52,23 +54,24 @@ def tile_picked_hashminmodhopmx_none_p_kernel(
         scale_table = keep.tile([P, T], U8, name="scale_table", tag="early", align_bytes=64)
         nc.vector.memset(scale_table[:].bitcast(I32), 0)
         offs_t = load_list(offs, "offs_t")
+        gain = keep.tile([P, PACK], F32, name="gain")
+        nc.sync.dma_start(gain[:], gn.rearrange("(p t) o -> p (t o)", t=PACK))
         n1_t = load_list(n1, "n1_t")
-        n2_t = load_list(n2, "n2_t")
-        n3_t = load_list(n3, "n3_t")
-        n4_t = load_list(n4, "n4_t")
         nc.sync.dma_start(scale_table[:].bitcast(I32)[0:P:8, :], x_scales[0].bitcast(I32))
         w1_raw = keep.tile([P, PACK, H], F32, name="w1_raw", tag="w_raw")
         nc.sync.dma_start(w1_raw[:], w1.rearrange("(p j) c -> p j c", j=PACK))
         word_table = keep.tile([P, T], U32, name="word_table")
         nc.sync.dma_start(word_table[:].bitcast(I32), x_words[0].rearrange("p n t -> p (n t)").bitcast(I32))
+        n2_t = load_list(n2, "n2_t")
+        n3_t = load_list(n3, "n3_t")
+        n4_t = load_list(n4, "n4_t")
 
-        warm_in = keep.tile([P, 1], F32, name="warm_in")
-        warm_out = keep.tile([P, 1], F32, name="warm_out")
-        nc.gpsimd.memset(warm_in[:], 0.0)
-        nc.scalar.activation(warm_out[:], warm_in[:], COPY)
+        identity = keep.tile([P, P], F32, name="identity")
+        make_identity(nc, identity[:])
 
-        gain = keep.tile([P, PACK], F32, name="gain")
-        nc.sync.dma_start(gain[:], gn.rearrange("(p t) o -> p (t o)", t=PACK))
+
+        neg_gain = keep.tile([P, PACK], F32, name="neg_gain")
+        nc.scalar.activation(neg_gain[:], gain[:], COPY, scale=-1.0)
 
         picked_scales = keep.tile([P, S], U8, name="picked_scales")
         nc.vector.tensor_copy(picked_scales[:], scale_table[:].indirect(offs_t[:]))
@@ -84,8 +87,6 @@ def tile_picked_hashminmodhopmx_none_p_kernel(
         w1_grouped = keep.tile([P, PACK * H], BF16, name="w1_grouped", tag="early", align_bytes=64)
         deal_columns(nc.vector.tensor_copy, w1_grouped, w1_raw, 0, W1_VECTOR_SHARE)
         deal_columns(nc.scalar.copy, w1_grouped, w1_raw, W1_VECTOR_SHARE, P)
-        neg_gain = keep.tile([P, PACK], F32, name="neg_gain")
-        nc.scalar.activation(neg_gain[:], gain[:], COPY, scale=-1.0)
         w1_codes = keep.tile([P, H], U32, name="w1_codes", align_bytes=64)
         w1_plane = keep.tile([P, H], U8, name="w1_plane", align_bytes=64)
         nc.vector.quantize_mx(out=w1_codes[:].bitcast(FP8X4), scales=w1_plane[:], in_=w1_grouped[:])
@@ -101,7 +102,7 @@ def tile_picked_hashminmodhopmx_none_p_kernel(
         def product(bank, codes, plane, t, rhs, rhs_plane):
             nc.tensor.matmul_mx(
                 out=bank[:],
-                lhsT=codes[:, t * P : (t + 1) * P].bitcast(FP8X4),
+                lhsT=codes[t].bitcast(FP8X4),
                 lhsT_scale=plane[:, t * P : (t + 1) * P],
                 rhs=rhs.bitcast(FP8X4),
                 rhs_scale=rhs_plane,
@@ -129,14 +130,13 @@ def tile_picked_hashminmodhopmx_none_p_kernel(
 
         y_pos = [keep.tile([P, S], F32, name="y_pos%d" % t) for t in range(PACK)]
         project(
-            range(len(pieces)), w1_codes, w1_plane, x_codes, x_plane,
+            range(len(pieces)), [w1_codes[:, t * P : (t + 1) * P] for t in range(PACK)], w1_plane, x_codes, x_plane,
             lambda t: y_pos[t][:], lambda t: gain[:, t : t + 1], lambda t: neg_gain[:, t : t + 1],
         )
 
         w2_grouped = keep.tile([P, PACK * N], BF16, name="w2_grouped", align_bytes=64)
         deal_columns(nc.scalar.copy, w2_grouped, w2_raw, 0, P // 2)
         deal_columns(nc.scalar.copy, w2_grouped, w2_raw, P // 2, P)
-        w2_codes = keep.tile([P, N], U32, name="w2_codes", align_bytes=64)
         w2_plane = keep.tile([P, N], U8, name="w2_plane", align_bytes=64)
 
         def bf16_half(name, c):
@@ -144,7 +144,9 @@ def tile_picked_hashminmodhopmx_none_p_kernel(
 
         def round_and_interleave(name, c, planes):
             grouped = bf16_half(name, c)
-            nc.scalar.copy(grouped[:].rearrange("p (j t) -> p j t", t=PACK), planes.rearrange("p t j -> p j t"))
+            nc.scalar.copy(
+                grouped[:].rearrange("p (c i t) -> p c t i", i=PACK, t=PACK), planes.rearrange("p t (c i) -> p c t i", i=PACK)
+            )
             return grouped
 
         pa = keep.tile([P, PACK, S], F32, name="pa")
@@ -161,10 +163,14 @@ def tile_picked_hashminmodhopmx_none_p_kernel(
         b0 = round_and_interleave("b", 0, pb0[:])
         a1 = round_and_interleave("a", 1, pa[:, :, cols(1)])
 
-        def quantize_w2(lo, hi):
-            nc.vector.quantize_mx(
-                out=w2_codes[:, lo:hi].bitcast(FP8X4), scales=w2_plane[:, lo:hi], in_=w2_grouped[:, PACK * lo : PACK * hi]
-            )
+        w2_codes = {}
+
+        def quantize_w2(t0, t1, tag):
+            lo, hi = t0 * P, t1 * P
+            codes = keep.tile([P, hi - lo], U32, name="w2_codes", tag=tag, align_bytes=64)
+            nc.vector.quantize_mx(out=codes[:].bitcast(FP8X4), scales=w2_plane[:, lo:hi], in_=w2_grouped[:, PACK * lo : PACK * hi])
+            for t in range(t0, t1):
+                w2_codes[t] = codes[:, (t - t0) * P : (t - t0 + 1) * P]
 
         pb1 = keep.tile([P, PACK, HALF], F32, name="pb1", tag="w_raw")
         for t in range(PACK - 1):
@@ -172,7 +178,7 @@ def tile_picked_hashminmodhopmx_none_p_kernel(
 
         z_codes = keep.tile([P, S], U32, name="z_codes", align_bytes=64)
         z_plane = keep.tile([P, S], U8, name="z_plane", align_bytes=64)
-        st = [keep.tile([P, 2 * S], F32, name="st%d" % t) for t in range(PACK)]
+        st = [keep.tile([P, 2 * S], F32, name="st%d" % t) for t in range(PACK - 1)]
 
         def bound(name, c, b, op):
             res = bf16_half(name, c)
@@ -193,20 +199,21 @@ def tile_picked_hashminmodhopmx_none_p_kernel(
         low0 = bound("low", 0, b0, ALU.min)
         gather_pb(pb1, 1, PACK - 1)
         b1 = round_and_interleave("b", 1, pb1[:])
+        high1 = bf16_half("high", 1)
+        nc.scalar.activation(high1[:], b1[:], RELU)
         raised0 = combine("raised", 0, a0, low0, ALU.max)
         high0 = bound("high", 0, b0, ALU.max)
         z0 = combine("z", 0, raised0, high0, ALU.min)
-        quantize_w2(0, P)
+        quantize_w2(0, 1, "raised0")
         low1 = bound("low", 1, b1, ALU.min)
         quantize_z(0, z0)
         project_h([0])
         raised1 = combine("raised", 1, a1, low1, ALU.max)
-        high1 = bound("high", 1, b1, ALU.max)
         z1 = combine("z", 1, raised1, high1, ALU.min)
-        quantize_w2(P, 2 * P)
+        quantize_w2(1, 2, "low1")
         quantize_z(1, z1)
-        quantize_w2(2 * P, N)
-        project_h(range(1, len(pieces)))
+        quantize_w2(2, 4, "raised1")
+        project_h(range(1, len(pieces) - 1))
 
         out_rows = out.rearrange("(p t) j -> p t j", t=PACK)
         far = {}
@@ -214,8 +221,8 @@ def tile_picked_hashminmodhopmx_none_p_kernel(
         def difference(t):
             nc.vector.tensor_tensor(st[t][:, 0:S], negated[t][:].indirect(n3_t[:]), st[t][:, S : 2 * S], ALU.add)
 
-        def fetch(t, cs, offsets):
-            far[t, cs.start] = ring.tile([P, cs.stop - cs.start], F32, name="far")
+        def fetch(t, cs, offsets, tag):
+            far[t, cs.start] = keep.tile([P, cs.stop - cs.start], F32, name="far", tag=tag)
             nc.vector.tensor_copy(far[t, cs.start][:], st[t][:].indirect(offsets))
 
         def finish(t, cs):
@@ -223,16 +230,69 @@ def tile_picked_hashminmodhopmx_none_p_kernel(
             nc.vector.tensor_tensor(res[:], far[t, cs.start][:], st[t][:, cs], ALU.max)
             nc.sync.dma_start(out_rows[:, t, cs], res[:])
 
+        def copy_st(t):
+            twin = keep.tile([P, S], F32, name="twin%d" % t)
+            nc.sync.dma_start(twin[:], st[t][:, 0:S])
+            return twin
+
+        def excess(t, twin):
+            gap = keep.tile([P, S], F32, name="gap%d" % t)
+            nc.vector.tensor_tensor(gap[:], st[t][:].indirect(n4_t[:]), twin[:], ALU.subtract)
+            return gap
+
+        blocks = [slice(b * P, (b + 1) * P) for b in range(HALF // P)]
+
+        def turn_twin(t, c, twin, tag):
+            bank = psum.tile([P, HALF], F32, name="turned_bank", tag=tag)
+            for i, blk in enumerate(blocks):
+                nc.tensor.matmul(bank[:, blk], twin[:, cols(c)][:, blk], identity[:], start=(i == 0), stop=False, is_transpose=True)
+            return bank
+
+        def rectify(t, gap):
+            rise = keep.tile([P, S], F32, name="rise%d" % t)
+            nc.scalar.activation(rise[:], gap[:], RELU)
+            return rise
+
+        def add_rise(t, c, rise, bank):
+            for i, blk in enumerate(blocks):
+                nc.tensor.matmul(
+                    bank[:, blk], rise[:, cols(c)][:, blk], identity[:], start=False, stop=(i == len(blocks) - 1), is_transpose=True
+                )
+            turned = keep.tile([P, HALF], F32, name="turned%d%d" % (t, c))
+            nc.scalar.copy(turned[:], bank[:])
+            return turned
+
+        def turn_back(t, c, turned, tag):
+            bank = psum.tile([P, HALF], F32, name="back_bank", tag=tag)
+            for blk in blocks:
+                nc.tensor.transpose(bank[:, blk], turned[:, blk], identity[:])
+            res = keep.tile([P, HALF], F32, name="back%d%d" % (t, c))
+            nc.scalar.copy(res[:], bank[:])
+            nc.sync.dma_start(out_rows[:, t, cols(c)], res[:])
+
+        def finish_by_sums(t, rise, banks, tags):
+            turned = [add_rise(t, c, rise, banks[c]) for c in range(2)]
+            for c in range(2):
+                turn_back(t, c, turned[c], tags[c])
+
         whole = slice(0, S)
         difference(0)
-        for t in range(PACK - 1):
-            difference(t + 1)
-            if t > 0:
-                finish(t - 1, whole)
-            fetch(t, whole, n4_t[:])
-        last = PACK - 1
-        fetch(last, cols(0), half_list(n4_t, 0))
-        finish(last - 1, whole)
-        fetch(last, cols(1), half_list(n4_t, 1))
-        finish(last, cols(0))
-        finish(last, cols(1))
+        twin0 = copy_st(0)
+        difference(1)
+        twin1 = copy_st(1)
+        difference(2)
+        banks0 = [turn_twin(0, c, twin0, "bank%d" % (6 + c)) for c in range(2)]
+        banks1 = [turn_twin(1, c, twin1, "bank%d" % c) for c in range(2)]
+        rise0 = rectify(0, excess(0, twin0))
+        st.append(keep.tile([P, 2 * S], F32, name="st3", tag="st0"))
+        project_h([len(pieces) - 1])
+        rise1 = rectify(1, excess(1, twin1))
+        finish_by_sums(0, rise0, banks0, ["bank2", "bank3"])
+        finish_by_sums(1, rise1, banks1, ["bank4", "bank6"])
+        fetch(2, whole, n4_t[:], "st1")
+        difference(3)
+        finish(2, whole)
+        fetch(3, cols(0), half_list(n4_t, 0), "far_a")
+        fetch(3, cols(1), half_list(n4_t, 1), "far_b")
+        finish(3, cols(0))
+        finish(3, cols(1))

@@ -19,9 +19,20 @@ RELU = mybir.ActivationFunctionType.Relu
 
 P = 128
 PACK = 4
+BLOCK_ROWS = 8
+QUADRANT = 32
+LINE = 4
 HALF = S // 2
+QUARTER = S // 4
 LIST_COLS = S // 16
 W1_VECTOR_SHARE = 84
+
+SPARE_BANK = 6
+TILE0_FIRST_HALF = (0, slice(0, HALF), 0, False)
+TILE0_SECOND_HALF = [(0, slice(HALF, HALF + QUARTER), 1, False), (0, slice(HALF + QUARTER, S), 2, True)]
+TILE1_FIRST_HALF = (1, slice(0, HALF), SPARE_BANK, False)
+TILE1_SECOND_HALF = (1, slice(HALF, S), 3, False)
+WHOLE_TILE = {t: (t, slice(0, S), 2 + t, False) for t in range(1, PACK)}
 
 
 def deal_columns(engine_copy, grouped, raw, m0, m1):
@@ -31,13 +42,20 @@ def deal_columns(engine_copy, grouped, raw, m0, m1):
     )
 
 
+def cols(c):
+    return slice(c * HALF, (c + 1) * HALF)
+
+
+def half_list(tile, c):
+    return tile[:, c * LIST_COLS // 2 : (c + 1) * LIST_COLS // 2]
+
+
 def tile_picked_hashminmodhopmx_none_p_kernel(
     tc, x_words, x_scales, w1, gn, w2, offs, n1, n2, n3, n4, out
 ):
     nc = tc.nc
     with ExitStack() as ctx:
         keep = ctx.enter_context(tc.tile_pool(name="keep", bufs=1))
-        ring = ctx.enter_context(tc.tile_pool(name="ring", bufs=2))
         psum = ctx.enter_context(tc.psum_pool(name="psum", bufs=1))
 
         def load_list(src, name):
@@ -45,31 +63,25 @@ def tile_picked_hashminmodhopmx_none_p_kernel(
             nc.sync.dma_start(tile[:], src)
             return tile
 
-        def half_list(tile, c):
-            return tile[:, c * LIST_COLS // 2 : (c + 1) * LIST_COLS // 2]
-
-        def cols(c):
-            return slice(c * HALF, (c + 1) * HALF)
-
-        scale_table = keep.tile([P, T], U8, name="scale_table", tag="early", align_bytes=64)
+        scale_table = keep.tile([P, T], U8, name="scale_table", tag="scales_then_w1", align_bytes=64)
         nc.vector.memset(scale_table[:].bitcast(I32), 0)
+        w1_raw = keep.tile([P, PACK, H], F32, name="w1_raw", tag="staging")
+        w1_rows = w1.rearrange("(p j) c -> p j c", j=PACK)
+        nc.sync.dma_start(w1_raw[:, 0 : PACK // 2, :], w1_rows[:, 0 : PACK // 2, :])
         offs_t = load_list(offs, "offs_t")
         gain = keep.tile([P, PACK], F32, name="gain")
         nc.sync.dma_start(gain[:], gn.rearrange("(p t) o -> p (t o)", t=PACK))
+        nc.sync.dma_start(scale_table[:].bitcast(I32)[0:P:BLOCK_ROWS, :], x_scales[0].bitcast(I32))
         n1_t = load_list(n1, "n1_t")
-        nc.sync.dma_start(scale_table[:].bitcast(I32)[0:P:8, :], x_scales[0].bitcast(I32))
-        w1_raw = keep.tile([P, PACK, H], F32, name="w1_raw", tag="w_raw")
-        nc.sync.dma_start(w1_raw[:], w1.rearrange("(p j) c -> p j c", j=PACK))
+        n2_t = load_list(n2, "n2_t")
+        nc.sync.dma_start(w1_raw[:, PACK // 2 : PACK, :], w1_rows[:, PACK // 2 : PACK, :])
         word_table = keep.tile([P, T], U32, name="word_table")
         nc.sync.dma_start(word_table[:].bitcast(I32), x_words[0].rearrange("p n t -> p (n t)").bitcast(I32))
-        n2_t = load_list(n2, "n2_t")
         n3_t = load_list(n3, "n3_t")
         n4_t = load_list(n4, "n4_t")
 
         identity = keep.tile([P, P], F32, name="identity")
         make_identity(nc, identity[:])
-
-
         neg_gain = keep.tile([P, PACK], F32, name="neg_gain")
         nc.scalar.activation(neg_gain[:], gain[:], COPY, scale=-1.0)
 
@@ -77,14 +89,16 @@ def tile_picked_hashminmodhopmx_none_p_kernel(
         nc.vector.tensor_copy(picked_scales[:], scale_table[:].indirect(offs_t[:]))
         x_plane = keep.tile([P, S], U8, name="x_plane", align_bytes=64)
         nc.vector.memset(x_plane[:].bitcast(I32), 0)
-        for i in range(4):
-            nc.sync.dma_start(x_plane[:].bitcast(I32)[i:P:32, :], picked_scales[:].bitcast(I32)[8 * i : P : 32, :])
+        for i in range(QUADRANT // BLOCK_ROWS):
+            nc.sync.dma_start(
+                x_plane[:].bitcast(I32)[i:P:QUADRANT, :], picked_scales[:].bitcast(I32)[BLOCK_ROWS * i : P : QUADRANT, :]
+            )
 
         negated = [keep.tile([P, 2 * S], F32, name="negated%d" % t) for t in range(PACK)]
         for t in range(PACK):
             nc.vector.memset(negated[t][:, S : 2 * S], 0.0)
 
-        w1_grouped = keep.tile([P, PACK * H], BF16, name="w1_grouped", tag="early", align_bytes=64)
+        w1_grouped = keep.tile([P, PACK * H], BF16, name="w1_grouped", tag="scales_then_w1", align_bytes=64)
         deal_columns(nc.vector.tensor_copy, w1_grouped, w1_raw, 0, W1_VECTOR_SHARE)
         deal_columns(nc.scalar.copy, w1_grouped, w1_raw, W1_VECTOR_SHARE, P)
         w1_codes = keep.tile([P, H], U32, name="w1_codes", align_bytes=64)
@@ -95,20 +109,8 @@ def tile_picked_hashminmodhopmx_none_p_kernel(
         for c in range(2):
             nc.vector.tensor_copy(x_codes[:, cols(c)], word_table[:].indirect(half_list(offs_t, c)))
 
-        w2_raw = keep.tile([P, PACK, N], F32, name="w2_raw", tag="w_raw")
+        w2_raw = keep.tile([P, PACK, N], F32, name="w2_raw", tag="staging")
         nc.sync.dma_start(w2_raw[:], w2.rearrange("(p j) c -> p j c", j=PACK))
-
-
-        def product(bank, codes, plane, t, rhs, rhs_plane):
-            nc.tensor.matmul_mx(
-                out=bank[:],
-                lhsT=codes[t].bitcast(FP8X4),
-                lhsT_scale=plane[:, t * P : (t + 1) * P],
-                rhs=rhs.bitcast(FP8X4),
-                rhs_scale=rhs_plane,
-                start=True,
-                stop=True,
-            )
 
         def leave_bank(on_vector, dst, bank, factor):
             if on_vector:
@@ -116,28 +118,48 @@ def tile_picked_hashminmodhopmx_none_p_kernel(
             else:
                 nc.scalar.activation(dst, bank[:], COPY, scale=factor)
 
-        quarter = S // 4
-        pieces = [(0, slice(0, HALF), False), (0, slice(HALF, HALF + quarter), False), (0, slice(HALF + quarter, S), True)]
-        pieces = pieces + [(t, slice(0, S), False) for t in range(1, PACK)]
-
-        def project(which, codes, plane, rhs, rhs_plane, pos, pos_factor, neg_factor):
-            for b in which:
-                t, cs, on_vector = pieces[b]
+        def project(pieces, w_codes, w_plane, rhs_codes, rhs_plane, first, first_factor, second, second_factor):
+            for t, cs, b, on_vector in pieces:
                 bank = psum.tile([P, cs.stop - cs.start], F32, name="bank", tag="bank%d" % b)
-                product(bank, codes, plane, t, rhs[:, cs], rhs_plane[:, cs])
-                leave_bank(on_vector, negated[t][:, cs], bank, neg_factor(t))
-                leave_bank(on_vector, pos(t)[:, cs], bank, pos_factor(t))
+                nc.tensor.matmul_mx(
+                    out=bank[:],
+                    lhsT=w_codes[t].bitcast(FP8X4),
+                    lhsT_scale=w_plane[:, t * P : (t + 1) * P],
+                    rhs=rhs_codes[:, cs].bitcast(FP8X4),
+                    rhs_scale=rhs_plane[:, cs],
+                    start=True,
+                    stop=True,
+                )
+                leave_bank(on_vector, first(t)[:, cs], bank, first_factor(t))
+                leave_bank(False, second(t)[:, cs], bank, second_factor(t))
 
-        y_pos = [keep.tile([P, S], F32, name="y_pos%d" % t) for t in range(PACK)]
+        y_gained = [keep.tile([P, S], F32, name="y_gained%d" % t) for t in range(PACK)]
         project(
-            range(len(pieces)), [w1_codes[:, t * P : (t + 1) * P] for t in range(PACK)], w1_plane, x_codes, x_plane,
-            lambda t: y_pos[t][:], lambda t: gain[:, t : t + 1], lambda t: neg_gain[:, t : t + 1],
+            [TILE0_FIRST_HALF] + TILE0_SECOND_HALF + [WHOLE_TILE[t] for t in range(1, PACK)],
+            [w1_codes[:, t * P : (t + 1) * P] for t in range(PACK)],
+            w1_plane,
+            x_codes,
+            x_plane,
+            lambda t: y_gained[t][:],
+            lambda t: gain[:, t : t + 1],
+            lambda t: negated[t][:],
+            lambda t: neg_gain[:, t : t + 1],
         )
 
         w2_grouped = keep.tile([P, PACK * N], BF16, name="w2_grouped", align_bytes=64)
         deal_columns(nc.scalar.copy, w2_grouped, w2_raw, 0, P // 2)
         deal_columns(nc.scalar.copy, w2_grouped, w2_raw, P // 2, P)
         w2_plane = keep.tile([P, N], U8, name="w2_plane", align_bytes=64)
+        w2_codes = {}
+
+        def quantize_w2(t0, t1, tag):
+            lo, hi = t0 * P, t1 * P
+            codes = keep.tile([P, hi - lo], U32, name="w2_codes", tag=tag, align_bytes=64)
+            nc.vector.quantize_mx(
+                out=codes[:].bitcast(FP8X4), scales=w2_plane[:, lo:hi], in_=w2_grouped[:, PACK * lo : PACK * hi]
+            )
+            for t in range(t0, t1):
+                w2_codes[t] = codes[:, (t - t0) * P : (t - t0 + 1) * P]
 
         def bf16_half(name, c):
             return keep.tile([P, HALF * PACK], BF16, name="%s%d" % (name, c), align_bytes=64)
@@ -145,34 +167,27 @@ def tile_picked_hashminmodhopmx_none_p_kernel(
         def round_and_interleave(name, c, planes):
             grouped = bf16_half(name, c)
             nc.scalar.copy(
-                grouped[:].rearrange("p (c i t) -> p c t i", i=PACK, t=PACK), planes.rearrange("p t (c i) -> p c t i", i=PACK)
+                grouped[:].rearrange("p (c i t) -> p c t i", i=LINE, t=PACK),
+                planes.rearrange("p t (c i) -> p c t i", i=LINE),
             )
             return grouped
 
-        pa = keep.tile([P, PACK, S], F32, name="pa")
-        for t in range(PACK):
-            nc.vector.tensor_tensor(pa[:, t, :], negated[t][:].indirect(n1_t[:]), y_pos[t][:], ALU.add)
-
         def gather_pb(pb, c, t):
-            nc.vector.tensor_tensor(pb[:, t, :], y_pos[t][:].indirect(half_list(n2_t, c)), negated[t][:, cols(c)], ALU.add)
+            nc.vector.tensor_tensor(
+                pb[:, t, :], y_gained[t][:].indirect(half_list(n2_t, c)), negated[t][:, cols(c)], ALU.add
+            )
 
         pb0 = keep.tile([P, PACK, HALF], F32, name="pb0")
+        gather_pb(pb0, 0, 0)
+        pa = keep.tile([P, PACK, S], F32, name="pa")
         for t in range(PACK):
+            nc.vector.tensor_tensor(pa[:, t, :], negated[t][:].indirect(n1_t[:]), y_gained[t][:], ALU.add)
+        for t in range(1, PACK):
             gather_pb(pb0, 0, t)
         a0 = round_and_interleave("a", 0, pa[:, :, cols(0)])
         b0 = round_and_interleave("b", 0, pb0[:])
         a1 = round_and_interleave("a", 1, pa[:, :, cols(1)])
-
-        w2_codes = {}
-
-        def quantize_w2(t0, t1, tag):
-            lo, hi = t0 * P, t1 * P
-            codes = keep.tile([P, hi - lo], U32, name="w2_codes", tag=tag, align_bytes=64)
-            nc.vector.quantize_mx(out=codes[:].bitcast(FP8X4), scales=w2_plane[:, lo:hi], in_=w2_grouped[:, PACK * lo : PACK * hi])
-            for t in range(t0, t1):
-                w2_codes[t] = codes[:, (t - t0) * P : (t - t0 + 1) * P]
-
-        pb1 = keep.tile([P, PACK, HALF], F32, name="pb1", tag="w_raw")
+        pb1 = keep.tile([P, PACK, HALF], F32, name="pb1", tag="staging")
         for t in range(PACK - 1):
             gather_pb(pb1, 1, t)
 
@@ -180,7 +195,7 @@ def tile_picked_hashminmodhopmx_none_p_kernel(
         z_plane = keep.tile([P, S], U8, name="z_plane", align_bytes=64)
         st = [keep.tile([P, 2 * S], F32, name="st%d" % t) for t in range(PACK - 1)]
 
-        def bound(name, c, b, op):
+        def against_zero(name, c, b, op):
             res = bf16_half(name, c)
             nc.vector.tensor_scalar(res[:], b[:], 0.0, None, op)
             return res
@@ -193,62 +208,71 @@ def tile_picked_hashminmodhopmx_none_p_kernel(
         def quantize_z(c, z):
             nc.vector.quantize_mx(out=z_codes[:, cols(c)].bitcast(FP8X4), scales=z_plane[:, cols(c)], in_=z[:])
 
-        def project_h(which):
-            project(which, w2_codes, w2_plane, z_codes, z_plane, lambda t: st[t][:, S : 2 * S], lambda t: 1.0, lambda t: -1.0)
+        def project_h(pieces):
+            project(
+                pieces,
+                w2_codes,
+                w2_plane,
+                z_codes,
+                z_plane,
+                lambda t: negated[t][:],
+                lambda t: -1.0,
+                lambda t: st[t][:, S : 2 * S],
+                lambda t: 1.0,
+            )
 
-        low0 = bound("low", 0, b0, ALU.min)
+        low0 = against_zero("low", 0, b0, ALU.min)
         gather_pb(pb1, 1, PACK - 1)
         b1 = round_and_interleave("b", 1, pb1[:])
         high1 = bf16_half("high", 1)
         nc.scalar.activation(high1[:], b1[:], RELU)
+        high0 = against_zero("high", 0, b0, ALU.max)
         raised0 = combine("raised", 0, a0, low0, ALU.max)
-        high0 = bound("high", 0, b0, ALU.max)
+        quantize_w2(0, 2, "b0")
         z0 = combine("z", 0, raised0, high0, ALU.min)
-        quantize_w2(0, 1, "raised0")
-        low1 = bound("low", 1, b1, ALU.min)
+        low1 = against_zero("low", 1, b1, ALU.min)
         quantize_z(0, z0)
-        project_h([0])
+        project_h([TILE0_FIRST_HALF, TILE1_FIRST_HALF])
         raised1 = combine("raised", 1, a1, low1, ALU.max)
+        quantize_w2(2, 3, "b1")
         z1 = combine("z", 1, raised1, high1, ALU.min)
-        quantize_w2(1, 2, "low1")
         quantize_z(1, z1)
-        quantize_w2(2, 4, "raised1")
-        project_h(range(1, len(pieces) - 1))
+        quantize_w2(3, PACK, "z1")
+        project_h(TILE0_SECOND_HALF + [TILE1_SECOND_HALF, WHOLE_TILE[2]])
 
         out_rows = out.rearrange("(p t) j -> p t j", t=PACK)
-        far = {}
 
-        def difference(t):
-            nc.vector.tensor_tensor(st[t][:, 0:S], negated[t][:].indirect(n3_t[:]), st[t][:, S : 2 * S], ALU.add)
+        def difference(t, cs, offsets):
+            nc.vector.tensor_tensor(st[t][:, cs], negated[t][:].indirect(offsets), st[t][:, S : 2 * S][:, cs], ALU.add)
 
-        def fetch(t, cs, offsets, tag):
-            far[t, cs.start] = keep.tile([P, cs.stop - cs.start], F32, name="far", tag=tag)
-            nc.vector.tensor_copy(far[t, cs.start][:], st[t][:].indirect(offsets))
+        def fetch(t, width, offsets, tag):
+            far = keep.tile([P, width], F32, name="far", tag=tag)
+            nc.vector.tensor_copy(far[:], st[t][:].indirect(offsets))
+            return far
 
-        def finish(t, cs):
-            res = ring.tile([P, cs.stop - cs.start], F32, name="res", bufs=3)
-            nc.vector.tensor_tensor(res[:], far[t, cs.start][:], st[t][:, cs], ALU.max)
+        def finish_by_max(t, cs, far):
+            res = keep.tile([P, cs.stop - cs.start], F32, name="larger%d_%d" % (t, cs.start))
+            nc.vector.tensor_tensor(res[:], far[:], st[t][:, cs], ALU.max)
             nc.sync.dma_start(out_rows[:, t, cs], res[:])
+
+        blocks = [slice(b * P, (b + 1) * P) for b in range(HALF // P)]
 
         def copy_st(t):
             twin = keep.tile([P, S], F32, name="twin%d" % t)
             nc.sync.dma_start(twin[:], st[t][:, 0:S])
             return twin
 
-        def excess(t, twin):
-            gap = keep.tile([P, S], F32, name="gap%d" % t)
-            nc.vector.tensor_tensor(gap[:], st[t][:].indirect(n4_t[:]), twin[:], ALU.subtract)
-            return gap
-
-        blocks = [slice(b * P, (b + 1) * P) for b in range(HALF // P)]
-
-        def turn_twin(t, c, twin, tag):
+        def turn_twin(c, twin, tag):
             bank = psum.tile([P, HALF], F32, name="turned_bank", tag=tag)
             for i, blk in enumerate(blocks):
-                nc.tensor.matmul(bank[:, blk], twin[:, cols(c)][:, blk], identity[:], start=(i == 0), stop=False, is_transpose=True)
+                nc.tensor.matmul(
+                    bank[:, blk], twin[:, cols(c)][:, blk], identity[:], start=(i == 0), stop=False, is_transpose=True
+                )
             return bank
 
-        def rectify(t, gap):
+        def positive_excess(t, twin):
+            gap = keep.tile([P, S], F32, name="gap%d" % t)
+            nc.vector.tensor_tensor(gap[:], st[t][:].indirect(n4_t[:]), twin[:], ALU.subtract)
             rise = keep.tile([P, S], F32, name="rise%d" % t)
             nc.scalar.activation(rise[:], gap[:], RELU)
             return rise
@@ -256,7 +280,12 @@ def tile_picked_hashminmodhopmx_none_p_kernel(
         def add_rise(t, c, rise, bank):
             for i, blk in enumerate(blocks):
                 nc.tensor.matmul(
-                    bank[:, blk], rise[:, cols(c)][:, blk], identity[:], start=False, stop=(i == len(blocks) - 1), is_transpose=True
+                    bank[:, blk],
+                    rise[:, cols(c)][:, blk],
+                    identity[:],
+                    start=False,
+                    stop=(i == len(blocks) - 1),
+                    is_transpose=True,
                 )
             turned = keep.tile([P, HALF], F32, name="turned%d%d" % (t, c))
             nc.scalar.copy(turned[:], bank[:])
@@ -270,29 +299,29 @@ def tile_picked_hashminmodhopmx_none_p_kernel(
             nc.scalar.copy(res[:], bank[:])
             nc.sync.dma_start(out_rows[:, t, cols(c)], res[:])
 
-        def finish_by_sums(t, rise, banks, tags):
+        def finish_by_sums(t, rise, banks, back_tags):
             turned = [add_rise(t, c, rise, banks[c]) for c in range(2)]
             for c in range(2):
-                turn_back(t, c, turned[c], tags[c])
+                turn_back(t, c, turned[c], back_tags[c])
 
         whole = slice(0, S)
-        difference(0)
+        for c in range(2):
+            difference(0, cols(c), half_list(n3_t, c))
         twin0 = copy_st(0)
-        difference(1)
+        difference(1, whole, n3_t[:])
         twin1 = copy_st(1)
-        difference(2)
-        banks0 = [turn_twin(0, c, twin0, "bank%d" % (6 + c)) for c in range(2)]
-        banks1 = [turn_twin(1, c, twin1, "bank%d" % c) for c in range(2)]
-        rise0 = rectify(0, excess(0, twin0))
+        difference(2, whole, n3_t[:])
+        banks0 = [turn_twin(c, twin0, "bank%d" % (SPARE_BANK + c)) for c in range(2)]
+        banks1 = [turn_twin(c, twin1, "bank%d" % c) for c in range(2)]
+        rise0 = positive_excess(0, twin0)
         st.append(keep.tile([P, 2 * S], F32, name="st3", tag="st0"))
-        project_h([len(pieces) - 1])
-        rise1 = rectify(1, excess(1, twin1))
+        project_h([WHOLE_TILE[3]])
+        rise1 = positive_excess(1, twin1)
         finish_by_sums(0, rise0, banks0, ["bank2", "bank3"])
-        finish_by_sums(1, rise1, banks1, ["bank4", "bank6"])
-        fetch(2, whole, n4_t[:], "st1")
-        difference(3)
-        finish(2, whole)
-        fetch(3, cols(0), half_list(n4_t, 0), "far_a")
-        fetch(3, cols(1), half_list(n4_t, 1), "far_b")
-        finish(3, cols(0))
-        finish(3, cols(1))
+        finish_by_sums(1, rise1, banks1, ["bank4", "bank%d" % SPARE_BANK])
+        far2 = fetch(2, S, n4_t[:], "st1")
+        difference(3, whole, n3_t[:])
+        finish_by_max(2, whole, far2)
+        far3 = [fetch(3, HALF, half_list(n4_t, c), "far3_%d" % c) for c in range(2)]
+        for c in range(2):
+            finish_by_max(3, cols(c), far3[c])

from contextlib import ExitStack

import concourse.mybir as mybir
from concourse.masks import make_identity

K, T, S, H, N = 512, 2048, 512, 512, 512
FLOPS = 2 * K * H * S + 2 * H * N * S

F32 = mybir.dt.float32
BF16 = mybir.dt.bfloat16
I32 = mybir.dt.int32
U32 = mybir.dt.uint32
U16 = mybir.dt.uint16
U8 = mybir.dt.uint8
FP8X4 = mybir.dt.float8_e4m3fn_x4
ALU = mybir.AluOpType
COPY = mybir.ActivationFunctionType.Copy
RELU = mybir.ActivationFunctionType.Relu

P = 128
PACK = 4
BLOCK_ROWS = 8
QUADRANT = 32
LINE = 4
HALF = S // 2
QUARTER = S // 4
LIST_COLS = S // 16
W1_VECTOR_SHARE = 84

SPARE_BANK = 6
TILE0_FIRST_HALF = (0, slice(0, HALF), 0, False)
TILE0_SECOND_HALF = [(0, slice(HALF, HALF + QUARTER), 1, False), (0, slice(HALF + QUARTER, S), 2, True)]
TILE1_FIRST_HALF = (1, slice(0, HALF), SPARE_BANK, False)
TILE1_SECOND_HALF = (1, slice(HALF, S), 3, False)
WHOLE_TILE = {t: (t, slice(0, S), 2 + t, False) for t in range(1, PACK)}


def deal_columns(engine_copy, grouped, raw, m0, m1):
    engine_copy(
        grouped[:].rearrange("p (t m j) -> p m t j", t=PACK, j=PACK)[:, m0:m1],
        raw[:].rearrange("p j (m t) -> p m t j", t=PACK)[:, m0:m1],
    )


def cols(c):
    return slice(c * HALF, (c + 1) * HALF)


def half_list(tile, c):
    return tile[:, c * LIST_COLS // 2 : (c + 1) * LIST_COLS // 2]


def tile_picked_hashminmodhopmx_none_p_kernel(
    tc, x_words, x_scales, w1, gn, w2, offs, n1, n2, n3, n4, out
):
    nc = tc.nc
    with ExitStack() as ctx:
        keep = ctx.enter_context(tc.tile_pool(name="keep", bufs=1))
        psum = ctx.enter_context(tc.psum_pool(name="psum", bufs=1))

        def load_list(src, name):
            tile = keep.tile([P, LIST_COLS], U16, name=name)
            nc.sync.dma_start(tile[:], src)
            return tile

        scale_table = keep.tile([P, T], U8, name="scale_table", tag="scales_then_w1", align_bytes=64)
        nc.vector.memset(scale_table[:].bitcast(I32), 0)
        w1_raw = keep.tile([P, PACK, H], F32, name="w1_raw", tag="staging")
        w1_rows = w1.rearrange("(p j) c -> p j c", j=PACK)
        nc.sync.dma_start(w1_raw[:, 0 : PACK // 2, :], w1_rows[:, 0 : PACK // 2, :])
        offs_t = load_list(offs, "offs_t")
        gain = keep.tile([P, PACK], F32, name="gain")
        nc.sync.dma_start(gain[:], gn.rearrange("(p t) o -> p (t o)", t=PACK))
        nc.sync.dma_start(scale_table[:].bitcast(I32)[0:P:BLOCK_ROWS, :], x_scales[0].bitcast(I32))
        n1_t = load_list(n1, "n1_t")
        n2_t = load_list(n2, "n2_t")
        nc.sync.dma_start(w1_raw[:, PACK // 2 : PACK, :], w1_rows[:, PACK // 2 : PACK, :])
        word_table = keep.tile([P, T], U32, name="word_table")
        nc.sync.dma_start(word_table[:].bitcast(I32), x_words[0].rearrange("p n t -> p (n t)").bitcast(I32))
        n3_t = load_list(n3, "n3_t")
        n4_t = load_list(n4, "n4_t")

        identity = keep.tile([P, P], F32, name="identity")
        make_identity(nc, identity[:])
        neg_gain = keep.tile([P, PACK], F32, name="neg_gain")
        nc.scalar.activation(neg_gain[:], gain[:], COPY, scale=-1.0)

        picked_scales = keep.tile([P, S], U8, name="picked_scales")
        nc.vector.tensor_copy(picked_scales[:], scale_table[:].indirect(offs_t[:]))
        x_plane = keep.tile([P, S], U8, name="x_plane", align_bytes=64)
        nc.vector.memset(x_plane[:].bitcast(I32), 0)
        for i in range(QUADRANT // BLOCK_ROWS):
            nc.sync.dma_start(
                x_plane[:].bitcast(I32)[i:P:QUADRANT, :], picked_scales[:].bitcast(I32)[BLOCK_ROWS * i : P : QUADRANT, :]
            )

        negated = [keep.tile([P, 2 * S], F32, name="negated%d" % t) for t in range(PACK)]
        for t in range(PACK):
            nc.vector.memset(negated[t][:, S : 2 * S], 0.0)

        w1_grouped = keep.tile([P, PACK * H], BF16, name="w1_grouped", tag="scales_then_w1", align_bytes=64)
        deal_columns(nc.vector.tensor_copy, w1_grouped, w1_raw, 0, W1_VECTOR_SHARE)
        deal_columns(nc.scalar.copy, w1_grouped, w1_raw, W1_VECTOR_SHARE, P)
        w1_codes = keep.tile([P, H], U32, name="w1_codes", align_bytes=64)
        w1_plane = keep.tile([P, H], U8, name="w1_plane", align_bytes=64)
        nc.vector.quantize_mx(out=w1_codes[:].bitcast(FP8X4), scales=w1_plane[:], in_=w1_grouped[:])

        x_codes = keep.tile([P, S], U32, name="x_codes", align_bytes=64)
        for c in range(2):
            nc.vector.tensor_copy(x_codes[:, cols(c)], word_table[:].indirect(half_list(offs_t, c)))

        w2_raw = keep.tile([P, PACK, N], F32, name="w2_raw", tag="staging")
        nc.sync.dma_start(w2_raw[:], w2.rearrange("(p j) c -> p j c", j=PACK))

        def leave_bank(on_vector, dst, bank, factor):
            if on_vector:
                nc.vector.tensor_scalar(dst, bank[:], factor, None, ALU.mult)
            else:
                nc.scalar.activation(dst, bank[:], COPY, scale=factor)

        def project(pieces, w_codes, w_plane, rhs_codes, rhs_plane, first, first_factor, second, second_factor):
            for t, cs, b, on_vector in pieces:
                bank = psum.tile([P, cs.stop - cs.start], F32, name="bank", tag="bank%d" % b)
                nc.tensor.matmul_mx(
                    out=bank[:],
                    lhsT=w_codes[t].bitcast(FP8X4),
                    lhsT_scale=w_plane[:, t * P : (t + 1) * P],
                    rhs=rhs_codes[:, cs].bitcast(FP8X4),
                    rhs_scale=rhs_plane[:, cs],
                    start=True,
                    stop=True,
                )
                leave_bank(on_vector, first(t)[:, cs], bank, first_factor(t))
                leave_bank(False, second(t)[:, cs], bank, second_factor(t))

        y_gained = [keep.tile([P, S], F32, name="y_gained%d" % t) for t in range(PACK)]
        project(
            [TILE0_FIRST_HALF] + TILE0_SECOND_HALF + [WHOLE_TILE[t] for t in range(1, PACK)],
            [w1_codes[:, t * P : (t + 1) * P] for t in range(PACK)],
            w1_plane,
            x_codes,
            x_plane,
            lambda t: y_gained[t][:],
            lambda t: gain[:, t : t + 1],
            lambda t: negated[t][:],
            lambda t: neg_gain[:, t : t + 1],
        )

        w2_grouped = keep.tile([P, PACK * N], BF16, name="w2_grouped", align_bytes=64)
        deal_columns(nc.scalar.copy, w2_grouped, w2_raw, 0, P // 2)
        deal_columns(nc.scalar.copy, w2_grouped, w2_raw, P // 2, P)
        w2_plane = keep.tile([P, N], U8, name="w2_plane", align_bytes=64)
        w2_codes = {}

        def quantize_w2(t0, t1, tag):
            lo, hi = t0 * P, t1 * P
            codes = keep.tile([P, hi - lo], U32, name="w2_codes", tag=tag, align_bytes=64)
            nc.vector.quantize_mx(
                out=codes[:].bitcast(FP8X4), scales=w2_plane[:, lo:hi], in_=w2_grouped[:, PACK * lo : PACK * hi]
            )
            for t in range(t0, t1):
                w2_codes[t] = codes[:, (t - t0) * P : (t - t0 + 1) * P]

        def bf16_half(name, c):
            return keep.tile([P, HALF * PACK], BF16, name="%s%d" % (name, c), align_bytes=64)

        def round_and_interleave(name, c, planes):
            grouped = bf16_half(name, c)
            nc.scalar.copy(
                grouped[:].rearrange("p (c i t) -> p c t i", i=LINE, t=PACK),
                planes.rearrange("p t (c i) -> p c t i", i=LINE),
            )
            return grouped

        def gather_pb(pb, c, t):
            nc.vector.tensor_tensor(
                pb[:, t, :], y_gained[t][:].indirect(half_list(n2_t, c)), negated[t][:, cols(c)], ALU.add
            )

        pb0 = keep.tile([P, PACK, HALF], F32, name="pb0")
        gather_pb(pb0, 0, 0)
        pa = keep.tile([P, PACK, S], F32, name="pa")
        for t in range(PACK):
            nc.vector.tensor_tensor(pa[:, t, :], negated[t][:].indirect(n1_t[:]), y_gained[t][:], ALU.add)
        for t in range(1, PACK):
            gather_pb(pb0, 0, t)
        a0 = round_and_interleave("a", 0, pa[:, :, cols(0)])
        b0 = round_and_interleave("b", 0, pb0[:])
        a1 = round_and_interleave("a", 1, pa[:, :, cols(1)])
        pb1 = keep.tile([P, PACK, HALF], F32, name="pb1", tag="staging")
        for t in range(PACK - 1):
            gather_pb(pb1, 1, t)

        z_codes = keep.tile([P, S], U32, name="z_codes", align_bytes=64)
        z_plane = keep.tile([P, S], U8, name="z_plane", align_bytes=64)
        st = [keep.tile([P, 2 * S], F32, name="st%d" % t) for t in range(PACK - 1)]

        def against_zero(name, c, b, op):
            res = bf16_half(name, c)
            nc.vector.tensor_scalar(res[:], b[:], 0.0, None, op)
            return res

        def combine(name, c, x, y, op):
            res = bf16_half(name, c)
            nc.vector.tensor_tensor(res[:], x[:], y[:], op)
            return res

        def quantize_z(c, z):
            nc.vector.quantize_mx(out=z_codes[:, cols(c)].bitcast(FP8X4), scales=z_plane[:, cols(c)], in_=z[:])

        def project_h(pieces):
            project(
                pieces,
                w2_codes,
                w2_plane,
                z_codes,
                z_plane,
                lambda t: negated[t][:],
                lambda t: -1.0,
                lambda t: st[t][:, S : 2 * S],
                lambda t: 1.0,
            )

        low0 = against_zero("low", 0, b0, ALU.min)
        gather_pb(pb1, 1, PACK - 1)
        b1 = round_and_interleave("b", 1, pb1[:])
        high1 = bf16_half("high", 1)
        nc.scalar.activation(high1[:], b1[:], RELU)
        high0 = against_zero("high", 0, b0, ALU.max)
        raised0 = combine("raised", 0, a0, low0, ALU.max)
        quantize_w2(0, 2, "b0")
        z0 = combine("z", 0, raised0, high0, ALU.min)
        low1 = against_zero("low", 1, b1, ALU.min)
        quantize_z(0, z0)
        project_h([TILE0_FIRST_HALF, TILE1_FIRST_HALF])
        raised1 = combine("raised", 1, a1, low1, ALU.max)
        quantize_w2(2, 3, "b1")
        z1 = combine("z", 1, raised1, high1, ALU.min)
        quantize_z(1, z1)
        quantize_w2(3, PACK, "z1")
        project_h(TILE0_SECOND_HALF + [TILE1_SECOND_HALF, WHOLE_TILE[2]])

        out_rows = out.rearrange("(p t) j -> p t j", t=PACK)

        def difference(t, cs, offsets):
            nc.vector.tensor_tensor(st[t][:, cs], negated[t][:].indirect(offsets), st[t][:, S : 2 * S][:, cs], ALU.add)

        def fetch(t, width, offsets, tag):
            far = keep.tile([P, width], F32, name="far", tag=tag)
            nc.vector.tensor_copy(far[:], st[t][:].indirect(offsets))
            return far

        def finish_by_max(t, cs, far):
            res = keep.tile([P, cs.stop - cs.start], F32, name="larger%d_%d" % (t, cs.start))
            nc.vector.tensor_tensor(res[:], far[:], st[t][:, cs], ALU.max)
            nc.sync.dma_start(out_rows[:, t, cs], res[:])

        blocks = [slice(b * P, (b + 1) * P) for b in range(HALF // P)]

        def copy_st(t):
            twin = keep.tile([P, S], F32, name="twin%d" % t)
            nc.sync.dma_start(twin[:], st[t][:, 0:S])
            return twin

        def turn_twin(c, twin, tag):
            bank = psum.tile([P, HALF], F32, name="turned_bank", tag=tag)
            for i, blk in enumerate(blocks):
                nc.tensor.matmul(
                    bank[:, blk], twin[:, cols(c)][:, blk], identity[:], start=(i == 0), stop=False, is_transpose=True
                )
            return bank

        def positive_excess(t, twin):
            gap = keep.tile([P, S], F32, name="gap%d" % t)
            nc.vector.tensor_tensor(gap[:], st[t][:].indirect(n4_t[:]), twin[:], ALU.subtract)
            rise = keep.tile([P, S], F32, name="rise%d" % t)
            nc.scalar.activation(rise[:], gap[:], RELU)
            return rise

        def add_rise(t, c, rise, bank):
            for i, blk in enumerate(blocks):
                nc.tensor.matmul(
                    bank[:, blk],
                    rise[:, cols(c)][:, blk],
                    identity[:],
                    start=False,
                    stop=(i == len(blocks) - 1),
                    is_transpose=True,
                )
            turned = keep.tile([P, HALF], F32, name="turned%d%d" % (t, c))
            nc.scalar.copy(turned[:], bank[:])
            return turned

        def turn_back(t, c, turned, tag):
            bank = psum.tile([P, HALF], F32, name="back_bank", tag=tag)
            for blk in blocks:
                nc.tensor.transpose(bank[:, blk], turned[:, blk], identity[:])
            res = keep.tile([P, HALF], F32, name="back%d%d" % (t, c))
            nc.scalar.copy(res[:], bank[:])
            nc.sync.dma_start(out_rows[:, t, cols(c)], res[:])

        def finish_by_sums(t, rise, banks, back_tags):
            turned = [add_rise(t, c, rise, banks[c]) for c in range(2)]
            for c in range(2):
                turn_back(t, c, turned[c], back_tags[c])

        whole = slice(0, S)
        for c in range(2):
            difference(0, cols(c), half_list(n3_t, c))
        twin0 = copy_st(0)
        difference(1, whole, n3_t[:])
        twin1 = copy_st(1)
        difference(2, whole, n3_t[:])
        banks0 = [turn_twin(c, twin0, "bank%d" % (SPARE_BANK + c)) for c in range(2)]
        banks1 = [turn_twin(c, twin1, "bank%d" % c) for c in range(2)]
        rise0 = positive_excess(0, twin0)
        st.append(keep.tile([P, 2 * S], F32, name="st3", tag="st0"))
        project_h([WHOLE_TILE[3]])
        rise1 = positive_excess(1, twin1)
        finish_by_sums(0, rise0, banks0, ["bank2", "bank3"])
        finish_by_sums(1, rise1, banks1, ["bank4", "bank%d" % SPARE_BANK])
        far2 = fetch(2, S, n4_t[:], "st1")
        difference(3, whole, n3_t[:])
        finish_by_max(2, whole, far2)
        far3 = [fetch(3, HALF, half_list(n4_t, c), "far3_%d" % c) for c in range(2)]
        for c in range(2):
            finish_by_max(3, cols(c), far3[c])
